import numpy as np
import ml_dtypes


def mxq(x, axis, fmt="e4m3"):
    dtype, down = {"e4m3": (ml_dtypes.float8_e4m3fn, 7), "e5m2": (ml_dtypes.float8_e5m2, 14)}[fmt]
    v = np.moveaxis(np.asarray(x, np.float32).astype(ml_dtypes.bfloat16).astype(np.float64), axis, -1)
    blocks = v.reshape(v.shape[:-1] + (-1, 32))
    amax = np.abs(blocks).max(-1, keepdims=True)
    byte = np.maximum(np.where(amax > 0, np.frexp(amax)[1] - 1 + 127, 0) - down, 1)
    scale = np.exp2(byte - 127.0)
    codes = (blocks / scale).astype(np.float32).astype(dtype).astype(np.float64)
    return np.moveaxis((codes * scale).reshape(v.shape), -1, axis)


WIDE = False


def mx_kscale(k):
    if not WIDE:
        return np.ones(k)
    levels = np.array([10, -10, 5, -5, 0])
    if k % 512:
        return np.exp2(np.random.permutation(np.resize(levels, k // 32))).repeat(32)
    a = np.empty((k // 512, 16))
    for p in range(k // 512):
        a[p, :8] = np.random.permutation(np.resize(levels, 8))
        for g in range(8):
            far = levels[np.abs(levels - a[p, g]) >= 10]
            a[p, g + 8] = far[np.random.randint(len(far))]
    return np.exp2(a.ravel()).repeat(32)


def f64(x):
    return np.asarray(x).astype(np.float64)


def striped(idx):
    return np.tile(idx.reshape(-1, 16).T, (8, 1)).astype(np.uint16)


def unstriped(offs):
    return offs[:16].T.reshape(-1).astype(np.int64)


def striped8(idx):
    return np.concatenate([v.reshape(-1, 16).T for v in idx]).astype(np.uint16)


def unstriped8(offs):
    return np.stack([offs[16 * g:16 * g + 16].T.reshape(-1) for g in range(8)]).astype(np.int64)


E2M1 = np.array([0.0, 0.5, 1.0, 1.5, 2.0, 3.0, 4.0, 6.0, -0.0, -0.5, -1.0, -1.5, -2.0, -3.0, -4.0, -6.0])


def pack_weight(w, fmt):
    k, n = w.shape
    w = f64(np.asarray(w, np.float32).astype(ml_dtypes.bfloat16)).reshape(k // 32, 32, n)
    amax = np.abs(w).max(1)
    if fmt == "e4m3":
        byte = np.frexp(amax)[1] - 1 + 127 - 7
    else:
        mant, ex = np.frexp(amax / 6.0)
        byte = np.where(mant > 0.5, ex, ex - 1) + 127
    byte = np.clip(np.where(amax > 0, byte, 1), 1, 254)
    scaled = (w * np.exp2(127.0 - byte)[:, None, :]).reshape(k, n).astype(np.float32)
    by_word = np.ascontiguousarray(scaled.reshape(k // 512, 128, 4, n).transpose(0, 1, 3, 2))
    if fmt == "e4m3":
        words = by_word.astype(ml_dtypes.float8_e4m3fn).view(np.uint8)
    else:
        c = by_word.astype(ml_dtypes.float4_e2m1fn).view(np.uint8) & 0xF
        words = (c[..., 0::2] | (c[..., 1::2] << 4)).reshape(k // 512, 128, 2 * n)
    return np.ascontiguousarray(words), np.ascontiguousarray(byte.astype(np.uint8).reshape(k // 512, 16, n))


def unpack_weight(words, scales, fmt):
    g, _, n = scales.shape
    words = np.ascontiguousarray(words).reshape(g, 128, n, -1)
    if fmt == "e4m3":
        vals = words.view(ml_dtypes.float8_e4m3fn).astype(np.float64)
    else:
        nib = np.empty((g, 128, n, 4), np.uint8)
        nib[..., 0::2] = words & 0xF
        nib[..., 1::2] = words >> 4
        vals = E2M1[nib]
    vals = vals * np.repeat(np.exp2(scales.astype(np.float64) - 127.0), 8, axis=1)[..., None]
    return vals.transpose(0, 1, 3, 2).reshape(g * 512, n)


def pack_table(v):
    words, scales = pack_weight(v, "e4m3")
    return np.concatenate([words.reshape(words.shape[0], -1), scales.reshape(scales.shape[0], -1)], axis=1)


def unpack_table(tab):
    g, t = tab.shape[0], tab.shape[1] // 528
    return unpack_weight(tab[:, :512 * t].reshape(g, 128, t, 4), tab[:, 512 * t:].reshape(g, 16, t), "e4m3")


K, M, T, S = 1536, 128, 1024, 512


def setup_inputs():
    n = np.random.standard_normal
    s = mx_kscale(K)[:, None]
    u = mx_kscale(512)[:, None]
    p_w2 = pack_weight(1.4 * n((512, M)) / np.sqrt(512) / u, "e2m1")
    return {
        "tab": pack_table(n((K, T)) * s),
        "w1": (n((K, 512)) / np.sqrt(K) / s * u.T).astype(np.float32),
        "w2_words": p_w2[0],
        "w2_scales": p_w2[1],
        "b": (0.3 * n(128)).astype(np.float32),
        "wgo": np.repeat(np.random.uniform(0.5, 2.0, (8, S)), 16, axis=0).astype(np.float32),
        "offs": striped(np.random.permutation(T)[:S]),
        "offs2": striped8(np.stack([np.random.permutation(T)[:S] for _ in range(8)])),
    }


def reference(tab, w1, w2_words, w2_scales, b, wgo, offs, offs2):
    tab_ = unpack_table(tab)[:, unstriped(offs)]
    w1_ = mxq(f64(w1), 0, "e4m3")
    w2_ = unpack_weight(w2_words, w2_scales, "e2m1")
    h_ = mxq(np.maximum(w1_.T @ tab_, 0.0), 0, "e4m3")
    y = w2_.T @ h_
    place = unstriped8(offs2)[np.arange(M) % 128 // 16]
    out = np.zeros((M, T))
    out[np.arange(M)[:, None], place] = f64(wgo)[np.arange(M) % 128] * (y + f64(b)[:, None])
    return out

@@ -1,0 +1,172 @@
+from contextlib import ExitStack
+
+import concourse.mybir as mybir
+
+K, H, M, T, S = 1536, 512, 128, 1024, 512
+FLOPS = 2 * K * H * S + 2 * H * M * S
+
+F32 = mybir.dt.float32
+BF16 = mybir.dt.bfloat16
+I32 = mybir.dt.int32
+U32 = mybir.dt.uint32
+U16 = mybir.dt.uint16
+U8 = mybir.dt.uint8
+FP8X4 = mybir.dt.float8_e4m3fn_x4
+FP4X4 = mybir.dt.float4_e2m1fn_x4
+ACT = mybir.ActivationFunctionType
+MULT = mybir.AluOpType.mult
+
+P = 128
+PACK = 4
+K_PASS = P * PACK
+PASSES = K // K_PASS
+CHUNK = 128
+CHUNKS = S // CHUNK
+LIST_COLS = CHUNK // 16
+W1_ORDER = (1, 0, 2)
+
+
+def tile_list_tabhs_m_bias_kernel(tc, tab, w1, w2_words, w2_scales, b, wgo, offs, offs2, out):
+    nc = tc.nc
+    with ExitStack() as ctx:
+        keep = ctx.enter_context(tc.tile_pool(name="keep", bufs=1))
+        psum = ctx.enter_context(tc.psum_pool(name="psum", bufs=1))
+
+        pick = keep.tile([P, S // 16], U16, name="pick")
+        place = keep.tile([P, S // 16], U16, name="place")
+        tab_scales = keep.tile([P, T], U8, name="tab_scales", align_bytes=64)
+        w2_plane = keep.tile([P, M], U8, name="w2_plane", align_bytes=64)
+        w2_codes = keep.tile([P, 2 * M], U8, name="w2_codes", align_bytes=64)
+        page = keep.tile([P, T], F32, name="page", align_bytes=64)
+        bias = keep.tile([P, 1], F32, name="bias")
+        gain = keep.tile([P, S], F32, name="gain")
+        tab_words = [keep.tile([P, T], I32, name="tab_words%d" % a, align_bytes=64) for a in range(PASSES)]
+        w1_raw = [keep.tile([P, PACK, H], F32, name="w1_raw%d" % a, align_bytes=64) for a in range(PASSES)]
+
+        nc.gpsimd.memset(tab_scales[:].bitcast(I32), 0)
+        nc.vector.memset(w2_plane[:].bitcast(I32), 0)
+        nc.vector.memset(page[:], 0.0)
+
+        def load_words(a):
+            nc.sync.dma_start(tab_words[a][:], tab[a, 0:K_PASS * T].rearrange("(p n) -> p n", p=P).bitcast(I32))
+
+        def load_w1(a):
+            nc.sync.dma_start(w1_raw[a][:], w1[a * K_PASS:(a + 1) * K_PASS, :].rearrange("(p j) c -> p j c", j=PACK))
+
+        load_words(0)
+        nc.sync.dma_start(pick[:], offs)
+        for a in W1_ORDER:
+            load_w1(a)
+        load_words(1)
+        load_words(2)
+        nc.sync.dma_start(w2_codes[:].bitcast(I32), w2_words[0].bitcast(I32))
+        nc.sync.dma_start(gain[:], wgo)
+        nc.sync.dma_start(place[:], offs2)
+
+        for q in range(4):
+            rows = tab[:, (K_PASS + 4 * q) * T:(K_PASS + 4 * q + 4) * T].bitcast(I32)
+            nc.gpsimd.dma_start(tab_scales[32 * q:32 * q + 4 * PASSES, :].bitcast(I32),
+                                rows.rearrange("a (r n) -> a r n", r=4))
+        for q in range(4):
+            nc.gpsimd.dma_start(w2_plane[32 * q:32 * q + 4, :].bitcast(I32), w2_scales[0, 4 * q:4 * q + 4, :].bitcast(I32))
+        with nc.allow_non_contiguous_dma(reason="one bias value for each partition"):
+            nc.gpsimd.dma_start(bias[:], b.rearrange("(p o) -> p o", o=1))
+
+        picked = {}
+
+        def gather_words(a, first, count, tag):
+            words = keep.tile([P, count * CHUNK], U32, name="picked%d_%d" % (a, first), tag=tag, align_bytes=64)
+            nc.vector.tensor_copy(words[:], tab_words[a][:].bitcast(U32).indirect(pick[:, first * LIST_COLS:(first + count) * LIST_COLS]))
+            for i in range(count):
+                picked[a, first + i] = words[:, i * CHUNK:(i + 1) * CHUNK]
+
+        gather_words(0, 0, CHUNKS, "picked0")
+        picked_scales = keep.tile([P, S], U8, name="picked_scales", align_bytes=64)
+        nc.vector.tensor_copy(picked_scales[:], tab_scales[:].indirect(pick[:]))
+
+        w1_codes = {}
+        w1_planes = {}
+
+        def quantise_w1(a):
+            src = w1_raw[a][:].rearrange("p j (m t) -> p m j t", t=PACK)
+            halves = []
+            for u in range(2):
+                woven = keep.tile([P, 2, P, PACK], BF16, name="w1_woven%d_%d" % (a, u), align_bytes=64)
+                dst = woven[:].rearrange("p t m j -> p m j t")
+                if u == 0:
+                    nc.vector.tensor_copy(dst, src[:, :, :, 0:2])
+                else:
+                    nc.scalar.activation(dst, src[:, :, :, 2:4], ACT.Copy)
+                halves.append(woven)
+            for u in range(2):
+                codes = keep.tile([P, 2 * P], U32, name="w1_codes%d_%d" % (a, u), align_bytes=64)
+                plane = keep.tile([P, 2 * P], U8, name="w1_plane%d_%d" % (a, u), align_bytes=64)
+                nc.vector.quantize_mx(out=codes[:].bitcast(FP8X4), scales=plane[:],
+                                      in_=halves[u][:].rearrange("p t m j -> p (t m j)"))
+                w1_codes[a, u] = codes
+                w1_planes[a, u] = plane
+
+        for a in W1_ORDER:
+            quantise_w1(a)
+
+        banks = [psum.tile([P, PACK, CHUNK], F32, name="h_bank%d" % c) for c in range(CHUNKS)]
+
+        def first_product(c, a, last):
+            words = picked[a, c]
+            cols = slice(c * CHUNK, (c + 1) * CHUNK)
+            for t in range(PACK):
+                u, m_cols = t // 2, slice((t % 2) * P, (t % 2 + 1) * P)
+                nc.tensor.matmul_mx(out=banks[c][:, t, :],
+                                    lhsT=w1_codes[a, u][:, m_cols].bitcast(FP8X4), lhsT_scale=w1_planes[a, u][:, m_cols],
+                                    rhs=words.bitcast(FP8X4), rhs_scale=picked_scales[4 * a:P, cols],
+                                    start=(a == 0 and t == 0), stop=(last and t == PACK - 1))
+
+        for c in range(CHUNKS):
+            first_product(c, 0, False)
+        gather_words(1, 0, 2, "picked1_head")
+        for c in range(2):
+            first_product(c, 1, False)
+        for c in range(2):
+            gather_words(2, c, 1, "picked_ring" if c == 0 else "picked2_1")
+            first_product(c, 2, True)
+        gather_words(2, 2, 2, "picked2_tail")
+        for c in range(2, 4):
+            first_product(c, 2, False)
+        gather_words(1, 2, 1, "picked_ring")
+        first_product(2, 1, True)
+
+        h_woven = {}
+        y_sb = {}
+
+        def hidden(c):
+            h_woven[c] = keep.tile([P, CHUNK, PACK], BF16, name="h_woven%d" % c, tag="ring_a0" if c == 2 else "h_woven%d" % c, align_bytes=64)
+            nc.scalar.activation(h_woven[c][:], banks[c][:].rearrange("p t s -> p s t"), ACT.Relu)
+
+        def second_product(c):
+            codes = keep.tile([P, CHUNK], U32, name="h_codes%d" % c, tag="ring_a0" if c == 0 else "h_codes%d" % c, align_bytes=64)
+            plane = keep.tile([P, CHUNK], U8, name="h_plane%d" % c, tag="ring_c0" if c == 0 else "h_plane%d" % c, align_bytes=64)
+            nc.vector.quantize_mx(out=codes[:].bitcast(FP8X4), scales=plane[:], in_=h_woven[c][:].rearrange("p s t -> p (s t)"))
+            y_bank = psum.tile([P, CHUNK], F32, name="y_bank%d" % c)
+            nc.tensor.matmul_mx(out=y_bank[:], lhsT=w2_codes[:].bitcast(FP4X4), lhsT_scale=w2_plane[:],
+                                rhs=codes[:].bitcast(FP8X4), rhs_scale=plane[:], start=True, stop=True)
+            y_sb[c] = keep.tile([P, CHUNK], F32, name="y_sb%d" % c, align_bytes=64)
+            nc.scalar.activation(y_sb[c][:], y_bank[:], ACT.Identity, bias=bias[:])
+
+        def scatter(c):
+            nc.vector.tensor_tensor(page[:].indirect(place[:, c * LIST_COLS:(c + 1) * LIST_COLS]), y_sb[c][:],
+                                    gain[:, c * CHUNK:(c + 1) * CHUNK], MULT)
+
+        hidden(0)
+        hidden(1)
+        for c in range(CHUNKS):
+            second_product(c)
+            if c == 0:
+                gather_words(1, 3, 1, "ring_c0")
+                first_product(3, 1, True)
+            if c + 2 < CHUNKS:
+                hidden(c + 2)
+            if c >= 1:
+                scatter(c - 1)
+        scatter(CHUNKS - 1)
+
+        nc.sync.dma_start(out, page[:])

@@ -53,24 +53,26 @@ def tile_list_tabhs_m_bias_kernel(tc, tab, w1, w2_words, w2_scales, b, wgo, offs
         def load_w1(a):
             nc.sync.dma_start(w1_raw[a][:], w1[a * K_PASS:(a + 1) * K_PASS, :].rearrange("(p j) c -> p j c", j=PACK))
 
+        def load_tab_scales(q, queue):
+            rows = tab[:, (K_PASS + 4 * q) * T:(K_PASS + 4 * q + 4) * T].bitcast(I32)
+            queue.dma_start(tab_scales[32 * q:32 * q + 4 * PASSES, :].bitcast(I32), rows.rearrange("a (r n) -> a r n", r=4))
+
         load_words(0)
         nc.sync.dma_start(pick[:], offs)
-        for a in W1_ORDER:
+        load_w1(W1_ORDER[0])
+        for q in range(4):
+            load_tab_scales(q, nc.scalar if q < 2 else nc.sync)
+        for a in W1_ORDER[1:]:
             load_w1(a)
+        nc.sync.dma_start(place[:], offs2)
+        nc.sync.dma_start(w2_codes[:].bitcast(I32), w2_words[0].bitcast(I32))
         load_words(1)
         load_words(2)
-        nc.sync.dma_start(w2_codes[:].bitcast(I32), w2_words[0].bitcast(I32))
         nc.sync.dma_start(gain[:], wgo)
-        nc.sync.dma_start(place[:], offs2)
-
-        for q in range(4):
-            rows = tab[:, (K_PASS + 4 * q) * T:(K_PASS + 4 * q + 4) * T].bitcast(I32)
-            nc.gpsimd.dma_start(tab_scales[32 * q:32 * q + 4 * PASSES, :].bitcast(I32),
-                                rows.rearrange("a (r n) -> a r n", r=4))
-        for q in range(4):
-            nc.gpsimd.dma_start(w2_plane[32 * q:32 * q + 4, :].bitcast(I32), w2_scales[0, 4 * q:4 * q + 4, :].bitcast(I32))
         with nc.allow_non_contiguous_dma(reason="one bias value for each partition"):
-            nc.gpsimd.dma_start(bias[:], b.rearrange("(p o) -> p o", o=1))
+            nc.sync.dma_start(bias[:], b.rearrange("(p o) -> p o", o=1))
+        for q in range(4):
+            nc.sync.dma_start(w2_plane[32 * q:32 * q + 4, :].bitcast(I32), w2_scales[0, 4 * q:4 * q + 4, :].bitcast(I32))
 
         picked = {}
 
@@ -81,8 +83,6 @@ def tile_list_tabhs_m_bias_kernel(tc, tab, w1, w2_words, w2_scales, b, wgo, offs
                 picked[a, first + i] = words[:, i * CHUNK:(i + 1) * CHUNK]
 
         gather_words(0, 0, CHUNKS, "picked0")
-        picked_scales = keep.tile([P, S], U8, name="picked_scales", align_bytes=64)
-        nc.vector.tensor_copy(picked_scales[:], tab_scales[:].indirect(pick[:]))
 
         w1_codes = {}
         w1_planes = {}
@@ -91,7 +91,7 @@ def tile_list_tabhs_m_bias_kernel(tc, tab, w1, w2_words, w2_scales, b, wgo, offs
             src = w1_raw[a][:].rearrange("p j (m t) -> p m j t", t=PACK)
             halves = []
             for u in range(2):
-                woven = keep.tile([P, 2, P, PACK], BF16, name="w1_woven%d_%d" % (a, u), align_bytes=64)
+                woven = keep.tile([P, 2, P, PACK], BF16, name="w1_woven%d_%d" % (a, u), tag="ring_s" if (a, u) == (W1_ORDER[0], 1) else "w1_woven%d_%d" % (a, u), align_bytes=64)
                 dst = woven[:].rearrange("p t m j -> p m j t")
                 if u == 0:
                     nc.vector.tensor_copy(dst, src[:, :, :, 0:2])
@@ -106,7 +106,10 @@ def tile_list_tabhs_m_bias_kernel(tc, tab, w1, w2_words, w2_scales, b, wgo, offs
                 w1_codes[a, u] = codes
                 w1_planes[a, u] = plane
 
-        for a in W1_ORDER:
+        quantise_w1(W1_ORDER[0])
+        picked_scales = keep.tile([P, S], U8, name="picked_scales", tag="ring_s", align_bytes=64)
+        nc.vector.tensor_copy(picked_scales[:], tab_scales[:].indirect(pick[:]))
+        for a in W1_ORDER[1:]:
             quantise_w1(a)
 
         banks = [psum.tile([P, PACK, CHUNK], F32, name="h_bank%d" % c) for c in range(CHUNKS)]

@@ -43,7 +43,7 @@ def tile_list_tabhs_m_bias_kernel(tc, tab, w1, w2_words, w2_scales, b, wgo, offs
         tab_words = [keep.tile([P, T], I32, name="tab_words%d" % a, align_bytes=64) for a in range(PASSES)]
         w1_raw = [keep.tile([P, PACK, H], F32, name="w1_raw%d" % a, align_bytes=64) for a in range(PASSES)]
 
-        nc.gpsimd.memset(tab_scales[:].bitcast(I32), 0)
+        nc.vector.memset(tab_scales[:].bitcast(I32), 0)
         nc.vector.memset(w2_plane[:].bitcast(I32), 0)
         nc.vector.memset(page[:], 0.0)
 
@@ -126,14 +126,14 @@ def tile_list_tabhs_m_bias_kernel(tc, tab, w1, w2_words, w2_scales, b, wgo, offs
 
         for c in range(CHUNKS):
             first_product(c, 0, False)
-        gather_words(1, 0, 2, "picked1_head")
         for c in range(2):
+            gather_words(1, c, 1, "picked1_%d" % c)
             first_product(c, 1, False)
         for c in range(2):
             gather_words(2, c, 1, "picked_ring" if c == 0 else "picked2_1")
             first_product(c, 2, True)
-        gather_words(2, 2, 2, "picked2_tail")
         for c in range(2, 4):
+            gather_words(2, c, 1, "picked2_%d" % c)
             first_product(c, 2, False)
         gather_words(1, 2, 1, "picked_ring")
         first_product(2, 1, True)

@@ -20,10 +20,21 @@ P = 128
 PACK = 4
 K_PASS = P * PACK
 PASSES = K // K_PASS
+QUADRANT = 32
+QUADRANTS = P // QUADRANT
+SCALE_ROWS = 4
+GROUP = 16
 CHUNK = 128
 CHUNKS = S // CHUNK
-LIST_COLS = CHUNK // 16
+LIST_COLS = CHUNK // GROUP
+PAIR = 2
 W1_ORDER = (1, 0, 2)
+EARLY_CHUNKS = 2
+
+SCALES_AFTER_FIRST_W1 = "scales_after_first_w1"
+GATHER_2_AFTER_CHUNK_0 = "gather_2_after_chunk_0"
+GATHER_3_AFTER_Y_0 = "gather_3_after_y_0"
+RELU_2_AFTER_Y_0 = "relu_2_after_y_0"
 
 
 def tile_list_tabhs_m_bias_kernel(tc, tab, w1, w2_words, w2_scales, b, wgo, offs, offs2, out):
@@ -32,9 +43,9 @@ def tile_list_tabhs_m_bias_kernel(tc, tab, w1, w2_words, w2_scales, b, wgo, offs
         keep = ctx.enter_context(tc.tile_pool(name="keep", bufs=1))
         psum = ctx.enter_context(tc.psum_pool(name="psum", bufs=1))
 
-        pick = keep.tile([P, S // 16], U16, name="pick")
-        place = keep.tile([P, S // 16], U16, name="place")
-        tab_scales = keep.tile([P, T], U8, name="tab_scales", align_bytes=64)
+        pick = keep.tile([P, S // GROUP], U16, name="pick")
+        place = keep.tile([P, S // GROUP], U16, name="place")
+        tab_plane = keep.tile([P, T], U8, name="tab_plane", align_bytes=64)
         w2_plane = keep.tile([P, M], U8, name="w2_plane", align_bytes=64)
         w2_codes = keep.tile([P, 2 * M], U8, name="w2_codes", align_bytes=64)
         page = keep.tile([P, T], F32, name="page", align_bytes=64)
@@ -43,7 +54,7 @@ def tile_list_tabhs_m_bias_kernel(tc, tab, w1, w2_words, w2_scales, b, wgo, offs
         tab_words = [keep.tile([P, T], I32, name="tab_words%d" % a, align_bytes=64) for a in range(PASSES)]
         w1_raw = [keep.tile([P, PACK, H], F32, name="w1_raw%d" % a, align_bytes=64) for a in range(PASSES)]
 
-        nc.vector.memset(tab_scales[:].bitcast(I32), 0)
+        nc.vector.memset(tab_plane[:].bitcast(I32), 0)
         nc.vector.memset(w2_plane[:].bitcast(I32), 0)
         nc.vector.memset(page[:], 0.0)
 
@@ -53,123 +64,125 @@ def tile_list_tabhs_m_bias_kernel(tc, tab, w1, w2_words, w2_scales, b, wgo, offs
         def load_w1(a):
             nc.sync.dma_start(w1_raw[a][:], w1[a * K_PASS:(a + 1) * K_PASS, :].rearrange("(p j) c -> p j c", j=PACK))
 
-        def load_tab_scales(q, queue):
-            rows = tab[:, (K_PASS + 4 * q) * T:(K_PASS + 4 * q + 4) * T].bitcast(I32)
-            queue.dma_start(tab_scales[32 * q:32 * q + 4 * PASSES, :].bitcast(I32), rows.rearrange("a (r n) -> a r n", r=4))
+        def load_tab_plane(q, queue):
+            first = K_PASS + SCALE_ROWS * q
+            rows = tab[:, first * T:(first + SCALE_ROWS) * T].bitcast(I32)
+            queue.dma_start(tab_plane[QUADRANT * q:QUADRANT * q + SCALE_ROWS * PASSES, :].bitcast(I32),
+                            rows.rearrange("a (r n) -> a r n", r=SCALE_ROWS))
 
         load_words(0)
         nc.sync.dma_start(pick[:], offs)
         load_w1(W1_ORDER[0])
-        for q in range(4):
-            load_tab_scales(q, nc.scalar if q < 2 else nc.sync)
+        for q in range(QUADRANTS):
+            load_tab_plane(q, nc.scalar if q < QUADRANTS // 2 else nc.sync)
         for a in W1_ORDER[1:]:
             load_w1(a)
-        nc.sync.dma_start(place[:], offs2)
-        nc.sync.dma_start(w2_codes[:].bitcast(I32), w2_words[0].bitcast(I32))
         load_words(1)
         load_words(2)
-        nc.sync.dma_start(gain[:], wgo)
+        nc.sync.dma_start(place[:], offs2)
+        nc.sync.dma_start(w2_codes[:].bitcast(I32), w2_words[0].bitcast(I32))
         with nc.allow_non_contiguous_dma(reason="one bias value for each partition"):
             nc.sync.dma_start(bias[:], b.rearrange("(p o) -> p o", o=1))
-        for q in range(4):
-            nc.sync.dma_start(w2_plane[32 * q:32 * q + 4, :].bitcast(I32), w2_scales[0, 4 * q:4 * q + 4, :].bitcast(I32))
+        for q in range(QUADRANTS):
+            nc.sync.dma_start(w2_plane[QUADRANT * q:QUADRANT * q + SCALE_ROWS, :].bitcast(I32),
+                              w2_scales[0, SCALE_ROWS * q:SCALE_ROWS * (q + 1), :].bitcast(I32))
+        nc.sync.dma_start(gain[:], wgo)
 
         picked = {}
 
-        def gather_words(a, first, count, tag):
-            words = keep.tile([P, count * CHUNK], U32, name="picked%d_%d" % (a, first), tag=tag, align_bytes=64)
-            nc.vector.tensor_copy(words[:], tab_words[a][:].bitcast(U32).indirect(pick[:, first * LIST_COLS:(first + count) * LIST_COLS]))
+        def gather_words(a, first, count, tag=None):
+            name = "picked%d_%d" % (a, first)
+            words = keep.tile([P, count * CHUNK], U32, name=name, tag=tag or name, align_bytes=64)
+            entries = pick[:, first * LIST_COLS:(first + count) * LIST_COLS]
+            nc.vector.tensor_copy(words[:], tab_words[a][:].bitcast(U32).indirect(entries))
             for i in range(count):
                 picked[a, first + i] = words[:, i * CHUNK:(i + 1) * CHUNK]
-
-        gather_words(0, 0, CHUNKS, "picked0")
 
         w1_codes = {}
         w1_planes = {}
 
-        def quantise_w1(a):
-            src = w1_raw[a][:].rearrange("p j (m t) -> p m j t", t=PACK)
-            halves = []
-            for u in range(2):
-                woven = keep.tile([P, 2, P, PACK], BF16, name="w1_woven%d_%d" % (a, u), tag="ring_s" if (a, u) == (W1_ORDER[0], 1) else "w1_woven%d_%d" % (a, u), align_bytes=64)
-                dst = woven[:].rearrange("p t m j -> p m j t")
-                if u == 0:
-                    nc.vector.tensor_copy(dst, src[:, :, :, 0:2])
-                else:
-                    nc.scalar.activation(dst, src[:, :, :, 2:4], ACT.Copy)
-                halves.append(woven)
-            for u in range(2):
-                codes = keep.tile([P, 2 * P], U32, name="w1_codes%d_%d" % (a, u), align_bytes=64)
-                plane = keep.tile([P, 2 * P], U8, name="w1_plane%d_%d" % (a, u), align_bytes=64)
+        def quantise_w1(a, scalar_tag=None):
+            source = w1_raw[a][:].rearrange("p j (m t) -> p m j t", t=PACK)
+            woven_vector = keep.tile([P, PAIR, P, PACK], BF16, name="w1_woven%d_0" % a, align_bytes=64)
+            nc.vector.tensor_copy(woven_vector[:].rearrange("p t m j -> p m j t"), source[:, :, :, 0:PAIR])
+            name = "w1_woven%d_1" % a
+            woven_scalar = keep.tile([P, PAIR, P, PACK], BF16, name=name, tag=scalar_tag or name, align_bytes=64)
+            nc.scalar.activation(woven_scalar[:].rearrange("p t m j -> p m j t"), source[:, :, :, PAIR:PACK], ACT.Copy)
+            for u, woven in enumerate((woven_vector, woven_scalar)):
+                codes = keep.tile([P, PAIR * P], U32, name="w1_codes%d_%d" % (a, u), align_bytes=64)
+                plane = keep.tile([P, PAIR * P], U8, name="w1_plane%d_%d" % (a, u), align_bytes=64)
                 nc.vector.quantize_mx(out=codes[:].bitcast(FP8X4), scales=plane[:],
-                                      in_=halves[u][:].rearrange("p t m j -> p (t m j)"))
+                                      in_=woven[:].rearrange("p t m j -> p (t m j)"))
                 w1_codes[a, u] = codes
                 w1_planes[a, u] = plane
 
-        quantise_w1(W1_ORDER[0])
-        picked_scales = keep.tile([P, S], U8, name="picked_scales", tag="ring_s", align_bytes=64)
-        nc.vector.tensor_copy(picked_scales[:], tab_scales[:].indirect(pick[:]))
+        gather_words(0, 0, CHUNKS)
+        quantise_w1(W1_ORDER[0], scalar_tag=SCALES_AFTER_FIRST_W1)
+        picked_plane = keep.tile([P, S], U8, name="picked_plane", tag=SCALES_AFTER_FIRST_W1, align_bytes=64)
+        nc.vector.tensor_copy(picked_plane[:], tab_plane[:].indirect(pick[:]))
         for a in W1_ORDER[1:]:
             quantise_w1(a)
 
-        banks = [psum.tile([P, PACK, CHUNK], F32, name="h_bank%d" % c) for c in range(CHUNKS)]
+        h_banks = [psum.tile([P, PACK, CHUNK], F32, name="h_bank%d" % c) for c in range(CHUNKS)]
 
         def first_product(c, a, last):
-            words = picked[a, c]
             cols = slice(c * CHUNK, (c + 1) * CHUNK)
             for t in range(PACK):
-                u, m_cols = t // 2, slice((t % 2) * P, (t % 2 + 1) * P)
-                nc.tensor.matmul_mx(out=banks[c][:, t, :],
+                u, m_cols = t // PAIR, slice((t % PAIR) * P, (t % PAIR + 1) * P)
+                nc.tensor.matmul_mx(out=h_banks[c][:, t, :],
                                     lhsT=w1_codes[a, u][:, m_cols].bitcast(FP8X4), lhsT_scale=w1_planes[a, u][:, m_cols],
-                                    rhs=words.bitcast(FP8X4), rhs_scale=picked_scales[4 * a:P, cols],
+                                    rhs=picked[a, c].bitcast(FP8X4), rhs_scale=picked_plane[SCALE_ROWS * a:P, cols],
                                     start=(a == 0 and t == 0), stop=(last and t == PACK - 1))
 
+        def gather_and_multiply(c, a, last, tag=None):
+            gather_words(a, c, 1, tag)
+            first_product(c, a, last)
+
         for c in range(CHUNKS):
-            first_product(c, 0, False)
-        for c in range(2):
-            gather_words(1, c, 1, "picked1_%d" % c)
-            first_product(c, 1, False)
-        for c in range(2):
-            gather_words(2, c, 1, "picked_ring" if c == 0 else "picked2_1")
-            first_product(c, 2, True)
-        for c in range(2, 4):
-            gather_words(2, c, 1, "picked2_%d" % c)
-            first_product(c, 2, False)
-        gather_words(1, 2, 1, "picked_ring")
-        first_product(2, 1, True)
+            first_product(c, 0, last=False)
+        for c in range(EARLY_CHUNKS):
+            gather_and_multiply(c, 1, last=False)
+        for c in range(EARLY_CHUNKS):
+            gather_and_multiply(c, 2, last=True, tag=GATHER_2_AFTER_CHUNK_0 if c == 0 else None)
+        for c in range(EARLY_CHUNKS, CHUNKS):
+            gather_and_multiply(c, 2, last=False)
+        gather_and_multiply(2, 1, last=True, tag=GATHER_2_AFTER_CHUNK_0)
 
         h_woven = {}
-        y_sb = {}
 
-        def hidden(c):
-            h_woven[c] = keep.tile([P, CHUNK, PACK], BF16, name="h_woven%d" % c, tag="ring_a0" if c == 2 else "h_woven%d" % c, align_bytes=64)
-            nc.scalar.activation(h_woven[c][:], banks[c][:].rearrange("p t s -> p s t"), ACT.Relu)
+        def relu(c, tag=None):
+            name = "h_woven%d" % c
+            h_woven[c] = keep.tile([P, CHUNK, PACK], BF16, name=name, tag=tag or name, align_bytes=64)
+            nc.scalar.activation(h_woven[c][:], h_banks[c][:].rearrange("p t s -> p s t"), ACT.Relu)
 
-        def second_product(c):
-            codes = keep.tile([P, CHUNK], U32, name="h_codes%d" % c, tag="ring_a0" if c == 0 else "h_codes%d" % c, align_bytes=64)
-            plane = keep.tile([P, CHUNK], U8, name="h_plane%d" % c, tag="ring_c0" if c == 0 else "h_plane%d" % c, align_bytes=64)
+        y_biased = {}
+
+        def second_product(c, codes_tag=None, plane_tag=None):
+            codes_name, plane_name = "h_codes%d" % c, "h_plane%d" % c
+            codes = keep.tile([P, CHUNK], U32, name=codes_name, tag=codes_tag or codes_name, align_bytes=64)
+            plane = keep.tile([P, CHUNK], U8, name=plane_name, tag=plane_tag or plane_name, align_bytes=64)
             nc.vector.quantize_mx(out=codes[:].bitcast(FP8X4), scales=plane[:], in_=h_woven[c][:].rearrange("p s t -> p (s t)"))
             y_bank = psum.tile([P, CHUNK], F32, name="y_bank%d" % c)
             nc.tensor.matmul_mx(out=y_bank[:], lhsT=w2_codes[:].bitcast(FP4X4), lhsT_scale=w2_plane[:],
                                 rhs=codes[:].bitcast(FP8X4), rhs_scale=plane[:], start=True, stop=True)
-            y_sb[c] = keep.tile([P, CHUNK], F32, name="y_sb%d" % c, align_bytes=64)
-            nc.scalar.activation(y_sb[c][:], y_bank[:], ACT.Identity, bias=bias[:])
+            y_biased[c] = keep.tile([P, CHUNK], F32, name="y_biased%d" % c, align_bytes=64)
+            nc.scalar.activation(y_biased[c][:], y_bank[:], ACT.Identity, bias=bias[:])
 
         def scatter(c):
-            nc.vector.tensor_tensor(page[:].indirect(place[:, c * LIST_COLS:(c + 1) * LIST_COLS]), y_sb[c][:],
-                                    gain[:, c * CHUNK:(c + 1) * CHUNK], MULT)
+            entries = place[:, c * LIST_COLS:(c + 1) * LIST_COLS]
+            nc.vector.tensor_tensor(page[:].indirect(entries), y_biased[c][:], gain[:, c * CHUNK:(c + 1) * CHUNK], MULT)
 
-        hidden(0)
-        hidden(1)
-        for c in range(CHUNKS):
+        relu(0)
+        relu(1)
+        second_product(0, codes_tag=RELU_2_AFTER_Y_0, plane_tag=GATHER_3_AFTER_Y_0)
+        gather_and_multiply(3, 1, last=True, tag=GATHER_3_AFTER_Y_0)
+        relu(2, tag=RELU_2_AFTER_Y_0)
+        second_product(1)
+        relu(3)
+        scatter(0)
+        for c in range(2, CHUNKS):
             second_product(c)
-            if c == 0:
-                gather_words(1, 3, 1, "ring_c0")
-                first_product(3, 1, True)
-            if c + 2 < CHUNKS:
-                hidden(c + 2)
-            if c >= 1:
-                scatter(c - 1)
+            scatter(c - 1)
         scatter(CHUNKS - 1)
 
         nc.sync.dma_start(out, page[:])

from contextlib import ExitStack

import concourse.mybir as mybir

K, H, M, T, S = 1536, 512, 128, 1024, 512
FLOPS = 2 * K * H * S + 2 * H * M * S

F32 = mybir.dt.float32
BF16 = mybir.dt.bfloat16
I32 = mybir.dt.int32
U32 = mybir.dt.uint32
U16 = mybir.dt.uint16
U8 = mybir.dt.uint8
FP8X4 = mybir.dt.float8_e4m3fn_x4
FP4X4 = mybir.dt.float4_e2m1fn_x4
ACT = mybir.ActivationFunctionType
MULT = mybir.AluOpType.mult

P = 128
PACK = 4
K_PASS = P * PACK
PASSES = K // K_PASS
QUADRANT = 32
QUADRANTS = P // QUADRANT
SCALE_ROWS = 4
GROUP = 16
CHUNK = 128
CHUNKS = S // CHUNK
LIST_COLS = CHUNK // GROUP
PAIR = 2
W1_ORDER = (1, 0, 2)
EARLY_CHUNKS = 2

SCALES_AFTER_FIRST_W1 = "scales_after_first_w1"
GATHER_2_AFTER_CHUNK_0 = "gather_2_after_chunk_0"
GATHER_3_AFTER_Y_0 = "gather_3_after_y_0"
RELU_2_AFTER_Y_0 = "relu_2_after_y_0"


def tile_list_tabhs_m_bias_kernel(tc, tab, w1, w2_words, w2_scales, b, wgo, offs, offs2, out):
    nc = tc.nc
    with ExitStack() as ctx:
        keep = ctx.enter_context(tc.tile_pool(name="keep", bufs=1))
        psum = ctx.enter_context(tc.psum_pool(name="psum", bufs=1))

        pick = keep.tile([P, S // GROUP], U16, name="pick")
        place = keep.tile([P, S // GROUP], U16, name="place")
        tab_plane = keep.tile([P, T], U8, name="tab_plane", align_bytes=64)
        w2_plane = keep.tile([P, M], U8, name="w2_plane", align_bytes=64)
        w2_codes = keep.tile([P, 2 * M], U8, name="w2_codes", align_bytes=64)
        page = keep.tile([P, T], F32, name="page", align_bytes=64)
        bias = keep.tile([P, 1], F32, name="bias")
        gain = keep.tile([P, S], F32, name="gain")
        tab_words = [keep.tile([P, T], I32, name="tab_words%d" % a, align_bytes=64) for a in range(PASSES)]
        w1_raw = [keep.tile([P, PACK, H], F32, name="w1_raw%d" % a, align_bytes=64) for a in range(PASSES)]

        nc.vector.memset(tab_plane[:].bitcast(I32), 0)
        nc.vector.memset(w2_plane[:].bitcast(I32), 0)
        nc.vector.memset(page[:], 0.0)

        def load_words(a):
            nc.sync.dma_start(tab_words[a][:], tab[a, 0:K_PASS * T].rearrange("(p n) -> p n", p=P).bitcast(I32))

        def load_w1(a):
            nc.sync.dma_start(w1_raw[a][:], w1[a * K_PASS:(a + 1) * K_PASS, :].rearrange("(p j) c -> p j c", j=PACK))

        def load_tab_plane(q, queue):
            first = K_PASS + SCALE_ROWS * q
            rows = tab[:, first * T:(first + SCALE_ROWS) * T].bitcast(I32)
            queue.dma_start(tab_plane[QUADRANT * q:QUADRANT * q + SCALE_ROWS * PASSES, :].bitcast(I32),
                            rows.rearrange("a (r n) -> a r n", r=SCALE_ROWS))

        load_words(0)
        nc.sync.dma_start(pick[:], offs)
        load_w1(W1_ORDER[0])
        for q in range(QUADRANTS):
            load_tab_plane(q, nc.scalar if q < QUADRANTS // 2 else nc.sync)
        for a in W1_ORDER[1:]:
            load_w1(a)
        load_words(1)
        load_words(2)
        nc.sync.dma_start(place[:], offs2)
        nc.sync.dma_start(w2_codes[:].bitcast(I32), w2_words[0].bitcast(I32))
        with nc.allow_non_contiguous_dma(reason="one bias value for each partition"):
            nc.sync.dma_start(bias[:], b.rearrange("(p o) -> p o", o=1))
        for q in range(QUADRANTS):
            nc.sync.dma_start(w2_plane[QUADRANT * q:QUADRANT * q + SCALE_ROWS, :].bitcast(I32),
                              w2_scales[0, SCALE_ROWS * q:SCALE_ROWS * (q + 1), :].bitcast(I32))
        nc.sync.dma_start(gain[:], wgo)

        picked = {}

        def gather_words(a, first, count, tag=None):
            name = "picked%d_%d" % (a, first)
            words = keep.tile([P, count * CHUNK], U32, name=name, tag=tag or name, align_bytes=64)
            entries = pick[:, first * LIST_COLS:(first + count) * LIST_COLS]
            nc.vector.tensor_copy(words[:], tab_words[a][:].bitcast(U32).indirect(entries))
            for i in range(count):
                picked[a, first + i] = words[:, i * CHUNK:(i + 1) * CHUNK]

        w1_codes = {}
        w1_planes = {}

        def quantise_w1(a, scalar_tag=None):
            source = w1_raw[a][:].rearrange("p j (m t) -> p m j t", t=PACK)
            woven_vector = keep.tile([P, PAIR, P, PACK], BF16, name="w1_woven%d_0" % a, align_bytes=64)
            nc.vector.tensor_copy(woven_vector[:].rearrange("p t m j -> p m j t"), source[:, :, :, 0:PAIR])
            name = "w1_woven%d_1" % a
            woven_scalar = keep.tile([P, PAIR, P, PACK], BF16, name=name, tag=scalar_tag or name, align_bytes=64)
            nc.scalar.activation(woven_scalar[:].rearrange("p t m j -> p m j t"), source[:, :, :, PAIR:PACK], ACT.Copy)
            for u, woven in enumerate((woven_vector, woven_scalar)):
                codes = keep.tile([P, PAIR * P], U32, name="w1_codes%d_%d" % (a, u), align_bytes=64)
                plane = keep.tile([P, PAIR * P], U8, name="w1_plane%d_%d" % (a, u), align_bytes=64)
                nc.vector.quantize_mx(out=codes[:].bitcast(FP8X4), scales=plane[:],
                                      in_=woven[:].rearrange("p t m j -> p (t m j)"))
                w1_codes[a, u] = codes
                w1_planes[a, u] = plane

        gather_words(0, 0, CHUNKS)
        quantise_w1(W1_ORDER[0], scalar_tag=SCALES_AFTER_FIRST_W1)
        picked_plane = keep.tile([P, S], U8, name="picked_plane", tag=SCALES_AFTER_FIRST_W1, align_bytes=64)
        nc.vector.tensor_copy(picked_plane[:], tab_plane[:].indirect(pick[:]))
        for a in W1_ORDER[1:]:
            quantise_w1(a)

        h_banks = [psum.tile([P, PACK, CHUNK], F32, name="h_bank%d" % c) for c in range(CHUNKS)]

        def first_product(c, a, last):
            cols = slice(c * CHUNK, (c + 1) * CHUNK)
            for t in range(PACK):
                u, m_cols = t // PAIR, slice((t % PAIR) * P, (t % PAIR + 1) * P)
                nc.tensor.matmul_mx(out=h_banks[c][:, t, :],
                                    lhsT=w1_codes[a, u][:, m_cols].bitcast(FP8X4), lhsT_scale=w1_planes[a, u][:, m_cols],
                                    rhs=picked[a, c].bitcast(FP8X4), rhs_scale=picked_plane[SCALE_ROWS * a:P, cols],
                                    start=(a == 0 and t == 0), stop=(last and t == PACK - 1))

        def gather_and_multiply(c, a, last, tag=None):
            gather_words(a, c, 1, tag)
            first_product(c, a, last)

        for c in range(CHUNKS):
            first_product(c, 0, last=False)
        for c in range(EARLY_CHUNKS):
            gather_and_multiply(c, 1, last=False)
        for c in range(EARLY_CHUNKS):
            gather_and_multiply(c, 2, last=True, tag=GATHER_2_AFTER_CHUNK_0 if c == 0 else None)
        for c in range(EARLY_CHUNKS, CHUNKS):
            gather_and_multiply(c, 2, last=False)
        gather_and_multiply(2, 1, last=True, tag=GATHER_2_AFTER_CHUNK_0)

        h_woven = {}

        def relu(c, tag=None):
            name = "h_woven%d" % c
            h_woven[c] = keep.tile([P, CHUNK, PACK], BF16, name=name, tag=tag or name, align_bytes=64)
            nc.scalar.activation(h_woven[c][:], h_banks[c][:].rearrange("p t s -> p s t"), ACT.Relu)

        y_biased = {}

        def second_product(c, codes_tag=None, plane_tag=None):
            codes_name, plane_name = "h_codes%d" % c, "h_plane%d" % c
            codes = keep.tile([P, CHUNK], U32, name=codes_name, tag=codes_tag or codes_name, align_bytes=64)
            plane = keep.tile([P, CHUNK], U8, name=plane_name, tag=plane_tag or plane_name, align_bytes=64)
            nc.vector.quantize_mx(out=codes[:].bitcast(FP8X4), scales=plane[:], in_=h_woven[c][:].rearrange("p s t -> p (s t)"))
            y_bank = psum.tile([P, CHUNK], F32, name="y_bank%d" % c)
            nc.tensor.matmul_mx(out=y_bank[:], lhsT=w2_codes[:].bitcast(FP4X4), lhsT_scale=w2_plane[:],
                                rhs=codes[:].bitcast(FP8X4), rhs_scale=plane[:], start=True, stop=True)
            y_biased[c] = keep.tile([P, CHUNK], F32, name="y_biased%d" % c, align_bytes=64)
            nc.scalar.activation(y_biased[c][:], y_bank[:], ACT.Identity, bias=bias[:])

        def scatter(c):
            entries = place[:, c * LIST_COLS:(c + 1) * LIST_COLS]
            nc.vector.tensor_tensor(page[:].indirect(entries), y_biased[c][:], gain[:, c * CHUNK:(c + 1) * CHUNK], MULT)

        relu(0)
        relu(1)
        second_product(0, codes_tag=RELU_2_AFTER_Y_0, plane_tag=GATHER_3_AFTER_Y_0)
        gather_and_multiply(3, 1, last=True, tag=GATHER_3_AFTER_Y_0)
        relu(2, tag=RELU_2_AFTER_Y_0)
        second_product(1)
        relu(3)
        scatter(0)
        for c in range(2, CHUNKS):
            second_product(c)
            scatter(c - 1)
        scatter(CHUNKS - 1)

        nc.sync.dma_start(out, page[:])
